import numpy as np
import ml_dtypes


def mxq(x, axis, fmt="e4m3"):
    dtype, down = {"e4m3": (ml_dtypes.float8_e4m3fn, 7), "e5m2": (ml_dtypes.float8_e5m2, 14)}[fmt]
    v = np.moveaxis(np.asarray(x, np.float32).astype(ml_dtypes.bfloat16).astype(np.float64), axis, -1)
    blocks = v.reshape(v.shape[:-1] + (-1, 32))
    amax = np.abs(blocks).max(-1, keepdims=True)
    byte = np.maximum(np.where(amax > 0, np.frexp(amax)[1] - 1 + 127, 0) - down, 1)
    scale = np.exp2(byte - 127.0)
    codes = (blocks / scale).astype(np.float32).astype(dtype).astype(np.float64)
    return np.moveaxis((codes * scale).reshape(v.shape), -1, axis)


WIDE = False


def mx_kscale(k):
    if not WIDE:
        return np.ones(k)
    levels = np.array([30, -30])
    if k % 512:
        return np.exp2(np.random.permutation(np.resize(levels, k // 32))).repeat(32)
    a = np.empty((k // 512, 16))
    for p in range(k // 512):
        a[p, :8] = np.random.permutation(np.resize(levels, 8))
        for g in range(8):
            far = levels[np.abs(levels - a[p, g]) >= 10]
            a[p, g + 8] = far[np.random.randint(len(far))]
    return np.exp2(a.ravel()).repeat(32)


def f64(x):
    return np.asarray(x).astype(np.float64)


def striped(idx):
    return np.tile(np.asarray(idx).reshape(-1, 16).T, (8, 1)).astype(np.uint16)


def unstriped(offs):
    return offs[:16].T.reshape(-1).astype(np.int64)


E2M1 = np.array([0.0, 0.5, 1.0, 1.5, 2.0, 3.0, 4.0, 6.0, -0.0, -0.5, -1.0, -1.5, -2.0, -3.0, -4.0, -6.0])


def pack_weight(w, fmt):
    k, n = w.shape
    w = f64(np.asarray(w, np.float32).astype(ml_dtypes.bfloat16)).reshape(k // 32, 32, n)
    amax = np.abs(w).max(1)
    if fmt in ("e4m3", "e5m2"):
        byte = np.frexp(amax)[1] - 1 + 127 - (7 if fmt == "e4m3" else 14)
    else:
        mant, ex = np.frexp(amax / 6.0)
        byte = np.where(mant > 0.5, ex, ex - 1) + 127
    byte = np.clip(np.where(amax > 0, byte, 1), 1, 254)
    scaled = (w * np.exp2(127.0 - byte)[:, None, :]).reshape(k, n).astype(np.float32)
    by_word = np.ascontiguousarray(scaled.reshape(k // 512, 128, 4, n).transpose(0, 1, 3, 2))
    if fmt in ("e4m3", "e5m2"):
        words = by_word.astype(ml_dtypes.float8_e4m3fn if fmt == "e4m3" else ml_dtypes.float8_e5m2).view(np.uint8)
    else:
        c = by_word.astype(ml_dtypes.float4_e2m1fn).view(np.uint8) & 0xF
        words = (c[..., 0::2] | (c[..., 1::2] << 4)).reshape(k // 512, 128, 2 * n)
    return np.ascontiguousarray(words), np.ascontiguousarray(byte.astype(np.uint8).reshape(k // 512, 16, n))


def unpack_weight(words, scales, fmt):
    g, _, n = scales.shape
    words = np.ascontiguousarray(words).reshape(g, 128, n, -1)
    if fmt in ("e4m3", "e5m2"):
        vals = words.view(ml_dtypes.float8_e4m3fn if fmt == "e4m3" else ml_dtypes.float8_e5m2).astype(np.float64)
    else:
        nib = np.empty((g, 128, n, 4), np.uint8)
        nib[..., 0::2] = words & 0xF
        nib[..., 1::2] = words >> 4
        vals = E2M1[nib]
    vals = vals * np.repeat(np.exp2(scales.astype(np.float64) - 127.0), 8, axis=1)[..., None]
    return vals.transpose(0, 1, 3, 2).reshape(g * 512, n)


K, T, J, N, S, L = 1024, 1024, 256, 256, 512, 512


def setup_inputs():
    n = np.random.standard_normal
    idx = np.random.permutation(T)[:J]
    idx2 = np.random.permutation(S)[:J]
    fk = mx_kscale(K)
    fl = mx_kscale(L)
    xtp = pack_weight(n((K, T)) * np.random.uniform(0.4, 1.6, (1, T)) / fk[:, None], "e2m1")
    wap = pack_weight(n((K, N)) * 1 / np.sqrt(K) * fk[:, None], "e2m1")
    wbp = pack_weight(n((L, N)) * 1 / np.sqrt(L) * fl[:, None], "e5m2")
    return {
        "xt_words": xtp[0],
        "xt_scales": xtp[1],
        "wa_words": wap[0],
        "wa_scales": wap[1],
        "xs": (n((L, S)) * np.random.uniform(0.4, 1.6, (1, S)) / fl[:, None]).astype(np.float32),
        "wb_words": wbp[0],
        "wb_scales": wbp[1],
        "bi": (np.random.uniform(-0.6, 0.6, (1, N))).astype(np.float32),
        "offs": striped(idx),
        "offs2": striped(idx2),
    }


def reference(xt_words, xt_scales, wa_words, wa_scales, xs, wb_words, wb_scales, bi, offs, offs2):
    idx = unstriped(offs)
    idx2 = unstriped(offs2)
    xtu = unpack_weight(xt_words, xt_scales, "e2m1")
    wau = unpack_weight(wa_words, wa_scales, "e2m1")
    wbu = unpack_weight(wb_words, wb_scales, "e5m2")
    xtidxg = xtu[:, idx]
    a = xtidxg.T @ wau
    xsidx2q = mxq(f64(xs)[:, idx2], 0, "e5m2")
    b0 = xsidx2q.T @ wbu
    b2 = b0 + f64(bi)
    sm = np.minimum(a, b2)
    y = np.maximum(a, b2) - 2.0 * np.mean(sm, axis=1, keepdims=True)
    return y

@@ -1,0 +1,166 @@
+from contextlib import ExitStack
+
+import concourse.mybir as mybir
+from concourse.masks import make_identity
+
+K, T, J, N, S, L = 1024, 1024, 256, 256, 512, 512
+FLOPS = 2 * J * N * (K + L)
+
+F32 = mybir.dt.float32
+BF16 = mybir.dt.bfloat16
+I32 = mybir.dt.int32
+U32 = mybir.dt.uint32
+U16 = mybir.dt.uint16
+U8 = mybir.dt.uint8
+E2M1 = mybir.dt.float4_e2m1fn_x4
+E5M2 = mybir.dt.float8_e5m2_x4
+ALU = mybir.AluOpType
+ACT = mybir.ActivationFunctionType
+
+P = 128
+PACK = 4
+PASSES = K // (P * PACK)
+HALVES = J // P
+SHRINK = 2.0 / N
+
+
+def load_scale_rows(queue, plane, scales):
+    for q in range(4):
+        queue.dma_start(
+            out=plane[32 * q : 32 * q + 4].bitcast(I32),
+            in_=scales[:, 4 * q : 4 * q + 4, :].rearrange("z r c -> r z c").bitcast(I32),
+        )
+
+
+def tile_list_rows_othertable_largerlesssmaller_kernel(
+    tc, xt_words, xt_scales, wa_words, wa_scales, xs, wb_words, wb_scales, bi, offs, offs2, out
+):
+    nc = tc.nc
+    with ExitStack() as ctx:
+        sb = ctx.enter_context(tc.tile_pool(name="sb", bufs=1))
+        ps = ctx.enter_context(tc.psum_pool(name="ps", bufs=1))
+
+        token_list = sb.tile([P, J // 16], U16, name="token_list")
+        entry_list = sb.tile([P, J // 16], U16, name="entry_list")
+        xt_plane = sb.tile([P, PASSES, T], U8, name="xt_plane", align_bytes=64)
+        wa_plane = sb.tile([P, PASSES, N], U8, name="wa_plane", align_bytes=64)
+        wb_plane = sb.tile([P, 1, N], U8, name="wb_plane", align_bytes=64)
+        nc.vector.memset(xt_plane[:].bitcast(I32), 0)
+        nc.gpsimd.memset(wa_plane[:].bitcast(I32), 0)
+        nc.vector.memset(wb_plane[:].bitcast(I32), 0)
+        identity = sb.tile([P, P], F32, name="identity")
+        make_identity(nc, identity[:])
+
+        xs_rows = xs.rearrange("(p t) s -> p t s", t=PACK)
+        xs_pairs = [sb.tile([P, 2, S], F32, name=f"xs_pair{u}", align_bytes=64) for u in range(2)]
+        nc.sync.dma_start(entry_list[:], offs2)
+        nc.sync.dma_start(out=xs_pairs[0][:], in_=xs_rows[:, 0:2, :])
+        nc.sync.dma_start(token_list[:], offs)
+        nc.sync.dma_start(out=xs_pairs[1][:], in_=xs_rows[:, 2:4, :])
+        load_scale_rows(nc.scalar, xt_plane, xt_scales)
+        load_scale_rows(nc.gpsimd, wa_plane, wa_scales)
+
+        xt_table = [sb.tile([P, T], U16, name=f"xt_table{z}", align_bytes=64) for z in range(PASSES)]
+        for z in range(PASSES):
+            nc.sync.dma_start(out=xt_table[z][:].bitcast(I32), in_=xt_words[z].bitcast(I32))
+        bias_cols = sb.tile([P, 2], F32, name="bias_cols")
+        nc.sync.dma_start(out=bias_cols[:], in_=bi.rearrange("o (p e) -> p (o e)", e=2))
+        wb_codes = sb.tile([P, N], U32, name="wb_codes", align_bytes=64)
+        nc.sync.dma_start(
+            out=wb_codes[:].bitcast(I32), in_=wb_words[0].rearrange("p n t -> p (n t)").bitcast(I32)
+        )
+        load_scale_rows(nc.sync, wb_plane, wb_scales)
+        wa_codes = sb.tile([P, PASSES, 2 * N], U8, name="wa_codes", align_bytes=64)
+        nc.sync.dma_start(
+            out=wa_codes[:].bitcast(I32), in_=wa_words.rearrange("z p b -> p z b").bitcast(I32)
+        )
+
+        picked = sb.tile([P, PACK, J], F32, name="picked", align_bytes=64)
+        for t in range(PACK):
+            nc.scalar.activation(
+                picked[:, t, :], xs_pairs[t // 2][:, t % 2, :].indirect(entry_list[:]), ACT.Copy
+            )
+
+        x_scales = [sb.tile([P, J], U8, name=f"x_scales{z}", align_bytes=64) for z in range(PASSES)]
+        for z in range(PASSES):
+            nc.vector.tensor_copy(x_scales[z][:], xt_plane[:, z, :].indirect(token_list[:]))
+
+        bias_ps = ps.tile([P, 2, P], F32, name="bias_ps")
+        for e in range(2):
+            nc.tensor.transpose(bias_ps[:, e, :], bias_cols[:, e : e + 1].to_broadcast([P, P]), identity[:])
+        bias = sb.tile([P, N], F32, name="bias")
+        nc.scalar.activation(
+            bias[:].rearrange("p (m e) -> p m e", e=2), bias_ps[:].rearrange("p e m -> p m e"), ACT.Copy, scale=SHRINK
+        )
+
+        woven = sb.tile([P, J, PACK], BF16, name="woven", align_bytes=64)
+        nc.vector.tensor_copy(
+            out=woven[:].rearrange("p (c i) t -> p c t i", i=4),
+            in_=picked[:].rearrange("p t (c i) -> p c t i", i=4),
+        )
+        x_codes = [sb.tile([P, J], U16, name=f"x_codes{z}", align_bytes=64) for z in range(PASSES)]
+        nc.vector.tensor_copy(x_codes[0][:], xt_table[0][:].indirect(token_list[:]))
+        s_codes = sb.tile([P, J], U32, name="s_codes", align_bytes=64)
+        s_scales = sb.tile([P, J], U8, name="s_scales", align_bytes=64)
+        nc.vector.quantize_mx(
+            out=s_codes[:].bitcast(E5M2), scales=s_scales[:], in_=woven[:].rearrange("p j t -> p (j t)")
+        )
+        nc.vector.tensor_copy(x_codes[1][:], xt_table[1][:].indirect(token_list[:]))
+
+        sums = sb.tile([P, 8 * 4 * HALVES], F32, name="sums")
+        b_rows, a_ps = [], []
+        for h in range(HALVES):
+            slots = slice(h * P, (h + 1) * P)
+            b_ps = ps.tile([P, N], F32, name=f"b_ps{h}")
+            nc.tensor.matmul_mx(
+                out=b_ps[:],
+                lhsT=s_codes[:, slots].bitcast(E5M2),
+                lhsT_scale=s_scales[:, slots],
+                rhs=wb_codes[:].bitcast(E5M2),
+                rhs_scale=wb_plane[:, 0, :],
+                start=True,
+                stop=True,
+            )
+            b_row = sb.tile([P, N], F32, name=f"b_row{h}")
+            nc.vector.scalar_tensor_tensor(
+                b_row[:], b_ps[:], SHRINK, bias[:], ALU.mult, ALU.add, accum_out=sums[:, 32 * h : 32 * h + 1]
+            )
+            b_rows.append(b_row)
+        for h in range(HALVES):
+            slots = slice(h * P, (h + 1) * P)
+            acc = ps.tile([P, N], F32, name=f"a_ps{h}")
+            for z in range(PASSES):
+                nc.tensor.matmul_mx(
+                    out=acc[:],
+                    lhsT=x_codes[z][:, slots].bitcast(E2M1),
+                    lhsT_scale=x_scales[z][:, slots],
+                    rhs=wa_codes[:, z, :].bitcast(E2M1),
+                    rhs_scale=wa_plane[:, z, :],
+                    start=(z == 0),
+                    stop=(z == PASSES - 1),
+                )
+            a_ps.append(acc)
+        larger = []
+        for h in range(HALVES):
+            a_row = sb.tile([P, N], F32, name=f"a_row{h}")
+            nc.scalar.activation(
+                a_row[:], a_ps[h][:], ACT.Copy, scale=SHRINK, accum_out=sums[:, 32 * h + 8 : 32 * h + 9]
+            )
+            big = sb.tile([P, N], F32, name=f"larger{h}")
+            nc.vector.scalar_tensor_tensor(
+                big[:], a_row[:], 1.0, b_rows[h][:], ALU.mult, ALU.max, accum_out=sums[:, 32 * h + 16 : 32 * h + 17]
+            )
+            larger.append(big)
+        for h in range(HALVES):
+            shift = sums[:, 32 * h + 24 : 32 * h + 25]
+            nc.vector.tensor_scalar(
+                shift,
+                sums[:, 32 * h + 16 : 32 * h + 17],
+                sums[:, 32 * h : 32 * h + 1],
+                sums[:, 32 * h + 8 : 32 * h + 9],
+                ALU.subtract,
+                ALU.subtract,
+            )
+            result = sb.tile([P, N], F32, name=f"result{h}")
+            nc.vector.tensor_scalar(result[:], larger[h][:], 1.0 / SHRINK, shift, ALU.mult, ALU.add)
+            nc.sync.dma_start(out=out[h * P : (h + 1) * P, :], in_=result[:])

@@ -1,7 +1,6 @@
 from contextlib import ExitStack
 
 import concourse.mybir as mybir
-from concourse.masks import make_identity
 
 K, T, J, N, S, L = 1024, 1024, 256, 256, 512, 512
 FLOPS = 2 * J * N * (K + L)
@@ -43,79 +42,99 @@ def tile_list_rows_othertable_largerlesssmaller_kernel(
         token_list = sb.tile([P, J // 16], U16, name="token_list")
         entry_list = sb.tile([P, J // 16], U16, name="entry_list")
         xt_plane = sb.tile([P, PASSES, T], U8, name="xt_plane", align_bytes=64)
-        wa_plane = sb.tile([P, PASSES, N], U8, name="wa_plane", align_bytes=64)
-        wb_plane = sb.tile([P, 1, N], U8, name="wb_plane", align_bytes=64)
+        w_planes = sb.tile([P, PASSES + 1, N], U8, name="w_planes", align_bytes=64)
+        wa_plane = w_planes[:, 0:PASSES, :]
+        wb_plane = w_planes[:, PASSES : PASSES + 1, :]
         nc.vector.memset(xt_plane[:].bitcast(I32), 0)
-        nc.gpsimd.memset(wa_plane[:].bitcast(I32), 0)
-        nc.vector.memset(wb_plane[:].bitcast(I32), 0)
+        nc.vector.memset(w_planes[:].bitcast(I32), 0)
+        offsets = sb.tile([P, P], F32, name="column_less_row")
+        nc.gpsimd.iota(offsets[:], [[1, P]], base=0, channel_multiplier=-1, allow_small_or_imprecise_dtypes=True)
         identity = sb.tile([P, P], F32, name="identity")
-        make_identity(nc, identity[:])
+        nc.vector.tensor_scalar(identity[:], offsets[:], 0.0, None, ALU.is_equal)
 
         xs_rows = xs.rearrange("(p t) s -> p t s", t=PACK)
         xs_pairs = [sb.tile([P, 2, S], F32, name=f"xs_pair{u}", align_bytes=64) for u in range(2)]
-        nc.sync.dma_start(entry_list[:], offs2)
-        nc.sync.dma_start(out=xs_pairs[0][:], in_=xs_rows[:, 0:2, :])
-        nc.sync.dma_start(token_list[:], offs)
-        nc.sync.dma_start(out=xs_pairs[1][:], in_=xs_rows[:, 2:4, :])
-        load_scale_rows(nc.scalar, xt_plane, xt_scales)
-        load_scale_rows(nc.gpsimd, wa_plane, wa_scales)
-
-        xt_table = [sb.tile([P, T], U16, name=f"xt_table{z}", align_bytes=64) for z in range(PASSES)]
-        for z in range(PASSES):
-            nc.sync.dma_start(out=xt_table[z][:].bitcast(I32), in_=xt_words[z].bitcast(I32))
-        bias_cols = sb.tile([P, 2], F32, name="bias_cols")
-        nc.sync.dma_start(out=bias_cols[:], in_=bi.rearrange("o (p e) -> p (o e)", e=2))
-        wb_codes = sb.tile([P, N], U32, name="wb_codes", align_bytes=64)
-        nc.sync.dma_start(
-            out=wb_codes[:].bitcast(I32), in_=wb_words[0].rearrange("p n t -> p (n t)").bitcast(I32)
-        )
-        load_scale_rows(nc.sync, wb_plane, wb_scales)
+        xt_table = [sb.tile([P, T], U16, name=f"xt_table{z}", tag=f"xt_table{z}", align_bytes=64) for z in range(PASSES)]
         wa_codes = sb.tile([P, PASSES, 2 * N], U8, name="wa_codes", align_bytes=64)
+        wb_codes = sb.tile([P, N], U32, name="wb_codes", align_bytes=64)
+        bias_cols = sb.tile([P, 2], F32, name="bias_cols")
+        nc.sync.dma_start(token_list[:], offs)
+        nc.sync.dma_start(out=xt_table[0][:].bitcast(I32), in_=xt_words[0].bitcast(I32))
+        nc.sync.dma_start(entry_list[:], offs2)
+        load_scale_rows(nc.sync, xt_plane, xt_scales)
+        for u in range(2):
+            nc.sync.dma_start(out=xs_pairs[u][:], in_=xs_rows[:, 2 * u : 2 * u + 2, :])
+        nc.sync.dma_start(out=xt_table[1][:].bitcast(I32), in_=xt_words[1].bitcast(I32))
         nc.sync.dma_start(
             out=wa_codes[:].bitcast(I32), in_=wa_words.rearrange("z p b -> p z b").bitcast(I32)
         )
+        load_scale_rows(nc.sync, wa_plane, wa_scales)
+        nc.sync.dma_start(out=bias_cols[:], in_=bi.rearrange("o (p e) -> p (o e)", e=2))
+        nc.sync.dma_start(
+            out=wb_codes[:].bitcast(I32), in_=wb_words[0].rearrange("p n t -> p (n t)").bitcast(I32)
+        )
+        load_scale_rows(nc.gpsimd, wb_plane, wb_scales)
 
-        picked = sb.tile([P, PACK, J], F32, name="picked", align_bytes=64)
-        for t in range(PACK):
-            nc.scalar.activation(
-                picked[:, t, :], xs_pairs[t // 2][:, t % 2, :].indirect(entry_list[:]), ACT.Copy
-            )
-
+        x_codes = [sb.tile([P, J], U16, name=f"x_codes{z}", align_bytes=64) for z in range(PASSES)]
+        nc.vector.tensor_copy(x_codes[0][:], xt_table[0][:].indirect(token_list[:]))
         x_scales = [sb.tile([P, J], U8, name=f"x_scales{z}", align_bytes=64) for z in range(PASSES)]
         for z in range(PASSES):
             nc.vector.tensor_copy(x_scales[z][:], xt_plane[:, z, :].indirect(token_list[:]))
+        picked = sb.tile([P, PACK, J], F32, name="picked", tag="picked", align_bytes=64)
+        for u in range(2):
+            nc.scalar.activation(picked[:, 2 * u, :], xs_pairs[u][:, 0, :].indirect(entry_list[:]), ACT.Copy)
+            nc.vector.tensor_copy(picked[:, 2 * u + 1, :], xs_pairs[u][:, 1, :].indirect(entry_list[:]))
+        a_ps = [ps.tile([P, N], F32, name=f"a_ps{h}") for h in range(HALVES)]
+
+        def token_pass(z):
+            for h in range(HALVES):
+                slots = slice(h * P, (h + 1) * P)
+                nc.tensor.matmul_mx(
+                    out=a_ps[h][:],
+                    lhsT=x_codes[z][:, slots].bitcast(E2M1),
+                    lhsT_scale=x_scales[z][:, slots],
+                    rhs=wa_codes[:, z, :].bitcast(E2M1),
+                    rhs_scale=wa_plane[:, z, :],
+                    start=(z == 0),
+                    stop=(z == PASSES - 1),
+                )
+
+        nc.vector.tensor_copy(x_codes[1][:], xt_table[1][:].indirect(token_list[:]))
+        token_pass(0)
+        token_pass(1)
+
+        woven = [
+            sb.tile([P, P, PACK], BF16, name="woven0", tag="xt_table1", align_bytes=64),
+            sb.tile([P, P, PACK], BF16, name="woven1", align_bytes=64),
+        ]
+        for h, copy in enumerate((nc.vector.tensor_copy, nc.scalar.copy)):
+            copy(
+                out=woven[h][:].rearrange("p (c i) t -> p c t i", i=4),
+                in_=picked[:, :, h * P : (h + 1) * P].rearrange("p t (c i) -> p c t i", i=4),
+            )
+        s_codes = [sb.tile([P, P], U32, name=f"s_codes{h}", align_bytes=64) for h in range(HALVES)]
+        s_scales = [sb.tile([P, P], U8, name=f"s_scales{h}", align_bytes=64) for h in range(HALVES)]
+        for h in range(HALVES):
+            nc.vector.quantize_mx(
+                out=s_codes[h][:].bitcast(E5M2), scales=s_scales[h][:], in_=woven[h][:].rearrange("p j t -> p (j t)")
+            )
 
         bias_ps = ps.tile([P, 2, P], F32, name="bias_ps")
         for e in range(2):
             nc.tensor.transpose(bias_ps[:, e, :], bias_cols[:, e : e + 1].to_broadcast([P, P]), identity[:])
-        bias = sb.tile([P, N], F32, name="bias")
+        bias = sb.tile([P, N], F32, name="bias", tag="picked", align_bytes=64)
         nc.scalar.activation(
             bias[:].rearrange("p (m e) -> p m e", e=2), bias_ps[:].rearrange("p e m -> p m e"), ACT.Copy, scale=SHRINK
         )
 
-        woven = sb.tile([P, J, PACK], BF16, name="woven", align_bytes=64)
-        nc.vector.tensor_copy(
-            out=woven[:].rearrange("p (c i) t -> p c t i", i=4),
-            in_=picked[:].rearrange("p t (c i) -> p c t i", i=4),
-        )
-        x_codes = [sb.tile([P, J], U16, name=f"x_codes{z}", align_bytes=64) for z in range(PASSES)]
-        nc.vector.tensor_copy(x_codes[0][:], xt_table[0][:].indirect(token_list[:]))
-        s_codes = sb.tile([P, J], U32, name="s_codes", align_bytes=64)
-        s_scales = sb.tile([P, J], U8, name="s_scales", align_bytes=64)
-        nc.vector.quantize_mx(
-            out=s_codes[:].bitcast(E5M2), scales=s_scales[:], in_=woven[:].rearrange("p j t -> p (j t)")
-        )
-        nc.vector.tensor_copy(x_codes[1][:], xt_table[1][:].indirect(token_list[:]))
-
         sums = sb.tile([P, 8 * 4 * HALVES], F32, name="sums")
-        b_rows, a_ps = [], []
+        b_rows = []
         for h in range(HALVES):
-            slots = slice(h * P, (h + 1) * P)
             b_ps = ps.tile([P, N], F32, name=f"b_ps{h}")
             nc.tensor.matmul_mx(
                 out=b_ps[:],
-                lhsT=s_codes[:, slots].bitcast(E5M2),
-                lhsT_scale=s_scales[:, slots],
+                lhsT=s_codes[h][:].bitcast(E5M2),
+                lhsT_scale=s_scales[h][:],
                 rhs=wb_codes[:].bitcast(E5M2),
                 rhs_scale=wb_plane[:, 0, :],
                 start=True,
@@ -126,20 +145,6 @@ def tile_list_rows_othertable_largerlesssmaller_kernel(
                 b_row[:], b_ps[:], SHRINK, bias[:], ALU.mult, ALU.add, accum_out=sums[:, 32 * h : 32 * h + 1]
             )
             b_rows.append(b_row)
-        for h in range(HALVES):
-            slots = slice(h * P, (h + 1) * P)
-            acc = ps.tile([P, N], F32, name=f"a_ps{h}")
-            for z in range(PASSES):
-                nc.tensor.matmul_mx(
-                    out=acc[:],
-                    lhsT=x_codes[z][:, slots].bitcast(E2M1),
-                    lhsT_scale=x_scales[z][:, slots],
-                    rhs=wa_codes[:, z, :].bitcast(E2M1),
-                    rhs_scale=wa_plane[:, z, :],
-                    start=(z == 0),
-                    stop=(z == PASSES - 1),
-                )
-            a_ps.append(acc)
         larger = []
         for h in range(HALVES):
             a_row = sb.tile([P, N], F32, name=f"a_row{h}")
@@ -162,5 +167,9 @@ def tile_list_rows_othertable_largerlesssmaller_kernel(
                 ALU.subtract,
             )
             result = sb.tile([P, N], F32, name=f"result{h}")
-            nc.vector.tensor_scalar(result[:], larger[h][:], 1.0 / SHRINK, shift, ALU.mult, ALU.add)
-            nc.sync.dma_start(out=out[h * P : (h + 1) * P, :], in_=result[:])
+            if h == 0:
+                nc.scalar.activation(result[:], larger[h][:], ACT.Identity, scale=1.0 / SHRINK, bias=shift)
+                nc.scalar.dma_start(out=out[h * P : (h + 1) * P, :], in_=result[:])
+            else:
+                nc.vector.tensor_scalar(result[:], larger[h][:], 1.0 / SHRINK, shift, ALU.mult, ALU.add)
+                nc.sync.dma_start(out=out[h * P : (h + 1) * P, :], in_=result[:])

from contextlib import ExitStack

import concourse.mybir as mybir

K, T, J, N, S, L = 1024, 1024, 256, 256, 512, 512
FLOPS = 2 * J * N * (K + L)

F32 = mybir.dt.float32
BF16 = mybir.dt.bfloat16
I32 = mybir.dt.int32
U32 = mybir.dt.uint32
U16 = mybir.dt.uint16
U8 = mybir.dt.uint8
E2M1 = mybir.dt.float4_e2m1fn_x4
E5M2 = mybir.dt.float8_e5m2_x4
ALU = mybir.AluOpType
ACT = mybir.ActivationFunctionType

P = 128
PACK = 4
PASSES = K // (P * PACK)
HALVES = J // P
SHRINK = 2.0 / N


def load_scale_rows(queue, plane, scales):
    for q in range(4):
        queue.dma_start(
            out=plane[32 * q : 32 * q + 4].bitcast(I32),
            in_=scales[:, 4 * q : 4 * q + 4, :].rearrange("z r c -> r z c").bitcast(I32),
        )


def tile_list_rows_othertable_largerlesssmaller_kernel(
    tc, xt_words, xt_scales, wa_words, wa_scales, xs, wb_words, wb_scales, bi, offs, offs2, out
):
    nc = tc.nc
    with ExitStack() as ctx:
        sb = ctx.enter_context(tc.tile_pool(name="sb", bufs=1))
        ps = ctx.enter_context(tc.psum_pool(name="ps", bufs=1))

        token_list = sb.tile([P, J // 16], U16, name="token_list")
        entry_list = sb.tile([P, J // 16], U16, name="entry_list")
        xt_plane = sb.tile([P, PASSES, T], U8, name="xt_plane", align_bytes=64)
        w_planes = sb.tile([P, PASSES + 1, N], U8, name="w_planes", align_bytes=64)
        wa_plane = w_planes[:, 0:PASSES, :]
        wb_plane = w_planes[:, PASSES : PASSES + 1, :]
        nc.vector.memset(xt_plane[:].bitcast(I32), 0)
        nc.vector.memset(w_planes[:].bitcast(I32), 0)
        offsets = sb.tile([P, P], F32, name="column_less_row")
        nc.gpsimd.iota(offsets[:], [[1, P]], base=0, channel_multiplier=-1, allow_small_or_imprecise_dtypes=True)
        identity = sb.tile([P, P], F32, name="identity")
        nc.vector.tensor_scalar(identity[:], offsets[:], 0.0, None, ALU.is_equal)

        xs_rows = xs.rearrange("(p t) s -> p t s", t=PACK)
        xs_pairs = [sb.tile([P, 2, S], F32, name=f"xs_pair{u}", align_bytes=64) for u in range(2)]
        xt_table = [sb.tile([P, T], U16, name=f"xt_table{z}", tag=f"xt_table{z}", align_bytes=64) for z in range(PASSES)]
        wa_codes = sb.tile([P, PASSES, 2 * N], U8, name="wa_codes", align_bytes=64)
        wb_codes = sb.tile([P, N], U32, name="wb_codes", align_bytes=64)
        bias_cols = sb.tile([P, 2], F32, name="bias_cols")
        nc.sync.dma_start(token_list[:], offs)
        nc.sync.dma_start(out=xt_table[0][:].bitcast(I32), in_=xt_words[0].bitcast(I32))
        nc.sync.dma_start(entry_list[:], offs2)
        load_scale_rows(nc.sync, xt_plane, xt_scales)
        for u in range(2):
            nc.sync.dma_start(out=xs_pairs[u][:], in_=xs_rows[:, 2 * u : 2 * u + 2, :])
        nc.sync.dma_start(out=xt_table[1][:].bitcast(I32), in_=xt_words[1].bitcast(I32))
        nc.sync.dma_start(
            out=wa_codes[:].bitcast(I32), in_=wa_words.rearrange("z p b -> p z b").bitcast(I32)
        )
        load_scale_rows(nc.sync, wa_plane, wa_scales)
        nc.sync.dma_start(out=bias_cols[:], in_=bi.rearrange("o (p e) -> p (o e)", e=2))
        nc.sync.dma_start(
            out=wb_codes[:].bitcast(I32), in_=wb_words[0].rearrange("p n t -> p (n t)").bitcast(I32)
        )
        load_scale_rows(nc.gpsimd, wb_plane, wb_scales)

        x_codes = [sb.tile([P, J], U16, name=f"x_codes{z}", align_bytes=64) for z in range(PASSES)]
        nc.vector.tensor_copy(x_codes[0][:], xt_table[0][:].indirect(token_list[:]))
        x_scales = [sb.tile([P, J], U8, name=f"x_scales{z}", align_bytes=64) for z in range(PASSES)]
        for z in range(PASSES):
            nc.vector.tensor_copy(x_scales[z][:], xt_plane[:, z, :].indirect(token_list[:]))
        picked = sb.tile([P, PACK, J], F32, name="picked", tag="picked", align_bytes=64)
        for u in range(2):
            nc.scalar.activation(picked[:, 2 * u, :], xs_pairs[u][:, 0, :].indirect(entry_list[:]), ACT.Copy)
            nc.vector.tensor_copy(picked[:, 2 * u + 1, :], xs_pairs[u][:, 1, :].indirect(entry_list[:]))
        a_ps = [ps.tile([P, N], F32, name=f"a_ps{h}") for h in range(HALVES)]

        def token_pass(z):
            for h in range(HALVES):
                slots = slice(h * P, (h + 1) * P)
                nc.tensor.matmul_mx(
                    out=a_ps[h][:],
                    lhsT=x_codes[z][:, slots].bitcast(E2M1),
                    lhsT_scale=x_scales[z][:, slots],
                    rhs=wa_codes[:, z, :].bitcast(E2M1),
                    rhs_scale=wa_plane[:, z, :],
                    start=(z == 0),
                    stop=(z == PASSES - 1),
                )

        nc.vector.tensor_copy(x_codes[1][:], xt_table[1][:].indirect(token_list[:]))
        token_pass(0)
        token_pass(1)

        woven = [
            sb.tile([P, P, PACK], BF16, name="woven0", tag="xt_table1", align_bytes=64),
            sb.tile([P, P, PACK], BF16, name="woven1", align_bytes=64),
        ]
        for h, copy in enumerate((nc.vector.tensor_copy, nc.scalar.copy)):
            copy(
                out=woven[h][:].rearrange("p (c i) t -> p c t i", i=4),
                in_=picked[:, :, h * P : (h + 1) * P].rearrange("p t (c i) -> p c t i", i=4),
            )
        s_codes = [sb.tile([P, P], U32, name=f"s_codes{h}", align_bytes=64) for h in range(HALVES)]
        s_scales = [sb.tile([P, P], U8, name=f"s_scales{h}", align_bytes=64) for h in range(HALVES)]
        for h in range(HALVES):
            nc.vector.quantize_mx(
                out=s_codes[h][:].bitcast(E5M2), scales=s_scales[h][:], in_=woven[h][:].rearrange("p j t -> p (j t)")
            )

        bias_ps = ps.tile([P, 2, P], F32, name="bias_ps")
        for e in range(2):
            nc.tensor.transpose(bias_ps[:, e, :], bias_cols[:, e : e + 1].to_broadcast([P, P]), identity[:])
        bias = sb.tile([P, N], F32, name="bias", tag="picked", align_bytes=64)
        nc.scalar.activation(
            bias[:].rearrange("p (m e) -> p m e", e=2), bias_ps[:].rearrange("p e m -> p m e"), ACT.Copy, scale=SHRINK
        )

        sums = sb.tile([P, 8 * 4 * HALVES], F32, name="sums")
        b_rows = []
        for h in range(HALVES):
            b_ps = ps.tile([P, N], F32, name=f"b_ps{h}")
            nc.tensor.matmul_mx(
                out=b_ps[:],
                lhsT=s_codes[h][:].bitcast(E5M2),
                lhsT_scale=s_scales[h][:],
                rhs=wb_codes[:].bitcast(E5M2),
                rhs_scale=wb_plane[:, 0, :],
                start=True,
                stop=True,
            )
            b_row = sb.tile([P, N], F32, name=f"b_row{h}")
            nc.vector.scalar_tensor_tensor(
                b_row[:], b_ps[:], SHRINK, bias[:], ALU.mult, ALU.add, accum_out=sums[:, 32 * h : 32 * h + 1]
            )
            b_rows.append(b_row)
        larger = []
        for h in range(HALVES):
            a_row = sb.tile([P, N], F32, name=f"a_row{h}")
            nc.scalar.activation(
                a_row[:], a_ps[h][:], ACT.Copy, scale=SHRINK, accum_out=sums[:, 32 * h + 8 : 32 * h + 9]
            )
            big = sb.tile([P, N], F32, name=f"larger{h}")
            nc.vector.scalar_tensor_tensor(
                big[:], a_row[:], 1.0, b_rows[h][:], ALU.mult, ALU.max, accum_out=sums[:, 32 * h + 16 : 32 * h + 17]
            )
            larger.append(big)
        for h in range(HALVES):
            shift = sums[:, 32 * h + 24 : 32 * h + 25]
            nc.vector.tensor_scalar(
                shift,
                sums[:, 32 * h + 16 : 32 * h + 17],
                sums[:, 32 * h : 32 * h + 1],
                sums[:, 32 * h + 8 : 32 * h + 9],
                ALU.subtract,
                ALU.subtract,
            )
            result = sb.tile([P, N], F32, name=f"result{h}")
            if h == 0:
                nc.scalar.activation(result[:], larger[h][:], ACT.Identity, scale=1.0 / SHRINK, bias=shift)
                nc.scalar.dma_start(out=out[h * P : (h + 1) * P, :], in_=result[:])
            else:
                nc.vector.tensor_scalar(result[:], larger[h][:], 1.0 / SHRINK, shift, ALU.mult, ALU.add)
                nc.sync.dma_start(out=out[h * P : (h + 1) * P, :], in_=result[:])
